import numpy as np
import ml_dtypes


def mxq(x, axis, fmt="e4m3"):
    dtype, down = {"e4m3": (ml_dtypes.float8_e4m3fn, 7), "e5m2": (ml_dtypes.float8_e5m2, 14)}[fmt]
    v = np.moveaxis(np.asarray(x, np.float32).astype(ml_dtypes.bfloat16).astype(np.float64), axis, -1)
    blocks = v.reshape(v.shape[:-1] + (-1, 32))
    amax = np.abs(blocks).max(-1, keepdims=True)
    byte = np.maximum(np.where(amax > 0, np.frexp(amax)[1] - 1 + 127, 0) - down, 1)
    scale = np.exp2(byte - 127.0)
    codes = (blocks / scale).astype(np.float32).astype(dtype).astype(np.float64)
    return np.moveaxis((codes * scale).reshape(v.shape), -1, axis)


WIDE = False


def mx_kscale(k):
    if not WIDE:
        return np.ones(k)
    levels = np.array([10, -10, 5, -5, 0])
    if k % 512:
        return np.exp2(np.random.permutation(np.resize(levels, k // 32))).repeat(32)
    a = np.empty((k // 512, 16))
    for p in range(k // 512):
        a[p, :8] = np.random.permutation(np.resize(levels, 8))
        for g in range(8):
            far = levels[np.abs(levels - a[p, g]) >= 10]
            a[p, g + 8] = far[np.random.randint(len(far))]
    return np.exp2(a.ravel()).repeat(32)


BF16 = ml_dtypes.bfloat16


def bf(x):
    return np.asarray(x, np.float32).astype(BF16)


def f64(x):
    return np.asarray(x).astype(np.float64)


E2M1 = np.array([0.0, 0.5, 1.0, 1.5, 2.0, 3.0, 4.0, 6.0, -0.0, -0.5, -1.0, -1.5, -2.0, -3.0, -4.0, -6.0])


def pack_weight(w, fmt):
    k, n = w.shape
    w = f64(bf(w)).reshape(k // 32, 32, n)
    amax = np.abs(w).max(1)
    if fmt == "e4m3":
        byte = np.frexp(amax)[1] - 1 + 127 - 7
    else:
        mant, ex = np.frexp(amax / 6.0)
        byte = np.where(mant > 0.5, ex, ex - 1) + 127
    byte = np.clip(np.where(amax > 0, byte, 1), 1, 254)
    scaled = (w * np.exp2(127.0 - byte)[:, None, :]).reshape(k, n).astype(np.float32)
    by_word = np.ascontiguousarray(scaled.reshape(k // 512, 128, 4, n).transpose(0, 1, 3, 2))
    if fmt == "e4m3":
        words = by_word.astype(ml_dtypes.float8_e4m3fn).view(np.uint8)
    else:
        c = by_word.astype(ml_dtypes.float4_e2m1fn).view(np.uint8) & 0xF
        words = c[..., 0::2] | (c[..., 1::2] << 4)
    return np.ascontiguousarray(words), np.ascontiguousarray(byte.astype(np.uint8).reshape(k // 512, 16, n))


def unpack_weight(words, scales, fmt):
    g, p, n, _ = words.shape
    if fmt == "e4m3":
        vals = np.ascontiguousarray(words).view(ml_dtypes.float8_e4m3fn).astype(np.float64)
    else:
        nib = np.empty((g, p, n, 4), np.uint8)
        nib[..., 0::2] = words & 0xF
        nib[..., 1::2] = words >> 4
        vals = E2M1[nib]
    vals = vals * np.repeat(np.exp2(scales.astype(np.float64) - 127.0), 8, axis=1)[..., None]
    return vals.transpose(0, 1, 3, 2).reshape(g * 512, n)

def planes(Y):
    n, m = Y.shape
    b = f64(bf(Y)).reshape(n // 32, 32, m)
    amax = np.abs(b).max(1)
    byte = np.clip(np.where(amax > 0, np.frexp(amax)[1] - 1 + 127 - 7, 1), 1, 254)
    codes = (b * np.exp2(127.0 - byte)[:, None, :]).reshape(n, m).astype(np.float32).astype(ml_dtypes.float8_e4m3fn).view(np.uint8)
    words = codes.reshape(n // 512, 128, 4, m).transpose(0, 1, 3, 2)
    return np.ascontiguousarray(words), np.ascontiguousarray(byte.astype(np.uint8).reshape(n // 512, 16, m))


N, D, K = 2048, 1024, 512


def scale_rows(gain, m):
    return gain[:, None] * m


def setup_inputs():
    s = mx_kscale(D)
    u = mx_kscale(N)
    x = bf(np.random.standard_normal((N, D)) * s)
    p_words, p_scales = pack_weight(np.random.standard_normal((D, D)) / np.sqrt(D) / s[:, None], "e4m3")
    beta_words, beta_scales = pack_weight(np.random.standard_normal((D, K)) / np.sqrt(D) / s[:, None], "e4m3")
    return {
        "x": x,
        "p_words": p_words,
        "p_scales": p_scales,
        "beta_words": beta_words,
        "beta_scales": beta_scales,
        "r": bf(np.random.uniform(0.5, 1.5, N) * u),
        "t": bf((1.0 + 0.3 * np.random.standard_normal(N)) / u),
        "v": bf(np.random.standard_normal((D, K)) / np.sqrt(D)),
        "psi": bf(np.random.uniform(0.05, 0.2, D)),
    }


def core(x, p_words, p_scales, beta_words, beta_scales, r, t, v, psi):
    n_cases = x.shape[0]
    xq = mxq(f64(x), 1, "e4m3")
    e0 = xq @ unpack_weight(p_words, p_scales, "e4m3")
    e = scale_rows(f64(r), e0)
    z0 = xq @ unpack_weight(beta_words, beta_scales, "e4m3")
    z = scale_rows(f64(t), z0)
    c = mxq(e, 0, "e4m3").T @ mxq(z, 0, "e4m3")
    return (c / n_cases - f64(v)) / f64(psi)[:, None]


def reference(x, p_words, p_scales, beta_words, beta_scales, r, t, v, psi):
    R_out = core(x, p_words, p_scales, beta_words, beta_scales, r, t, v, psi)
    words, scales = planes(R_out.T)
    return R_out, words, scales

@@ -1,0 +1,330 @@
+from contextlib import ExitStack
+
+import concourse.mybir as mybir
+from concourse.masks import make_identity
+
+N, D, K = 2048, 1024, 512
+FLOPS = 2 * N * D * (D + K) + 2 * N * D * K
+
+F32 = mybir.dt.float32
+BF16 = mybir.dt.bfloat16
+I32 = mybir.dt.int32
+U32 = mybir.dt.uint32
+U8 = mybir.dt.uint8
+FP8X4 = mybir.dt.float8_e4m3fn_x4
+COPY = mybir.ActivationFunctionType.Copy
+MULT = mybir.AluOpType.mult
+ADD = mybir.AluOpType.add
+SUB = mybir.AluOpType.subtract
+
+P = 128
+G = N // 512
+C = D // 512
+MT = D // P
+
+
+def tile_factoranalysisemloadinggradient_x2_kernel(
+    tc, x, p_words, p_scales, beta_words, beta_scales, r, t, v, psi, out, out_words, out_scales
+):
+    nc = tc.nc
+    with ExitStack() as ctx:
+        keep = ctx.enter_context(tc.tile_pool(name="keep", bufs=1))
+        work = ctx.enter_context(tc.tile_pool(name="work", bufs=2))
+        acc_pool = ctx.enter_context(tc.psum_pool(name="acc", bufs=6))
+        tr_pool = ctx.enter_context(tc.psum_pool(name="tr", bufs=2))
+        ctx.enter_context(tc.manual_schedule())
+
+        def kept(name, shape, dtype):
+            return keep.tile(shape, dtype, name=name, tag=name, align_bytes=256)
+
+        ident = kept("ident", [P, P], F32)
+        ident_bf = kept("ident_bf", [P, P], BF16)
+        wscale = kept("wscale", [P, C * (D + K)], U8)
+        psi_sb = kept("psi_sb", [P, P], BF16)
+        rt_bf = kept("rt_bf", [P, 2, 16], BF16)
+        rt = kept("rt", [P, 2, 16], F32)
+        pw = kept("pw", [P, C, D], U32)
+        bw = kept("bw", [P, C, K], U32)
+        rpsi = kept("rpsi", [P, MT], F32)
+        rpsi_n = kept("rpsi_n", [P, MT], F32)
+        v_sb = kept("v_sb", [P, MT, K], BF16)
+        vp = kept("vp", [P, MT, K], F32)
+        pcodes = kept("pcodes", [P, D], U32)
+        pscale = kept("pscale", [P, D], U8)
+
+        xv = x.rearrange("(g p t) k -> g p t k", g=G, t=4)
+        pv = p_words.rearrange("c p n t -> c p (n t)").bitcast(I32)
+        bv = beta_words.rearrange("c p n t -> c p (n t)").bitcast(I32)
+
+        xr = {}
+        for g in range(G):
+            for h in range(2):
+                xr[g, h] = kept("xr%d%d" % (g, h), [P, 2, D], BF16)
+
+        nc.gpsimd.memset(wscale[:].bitcast(I32), 0)
+        make_identity(nc, ident[:])
+        nc.gpsimd.dma_start(out=rt_bf[:, 0, :].rearrange("p (g t) -> p g t", t=4), in_=r.rearrange("(g p t) -> p g t", g=G, t=4))
+        nc.gpsimd.dma_start(out=rt_bf[:, 1, :].rearrange("p (g t) -> p g t", t=4), in_=t.rearrange("(g p t) -> p g t", g=G, t=4))
+        nc.gpsimd.memset(psi_sb[:], 0.0)
+        nc.gpsimd.dma_start(out=psi_sb[0:MT, :], in_=psi.rearrange("(m p) -> m p", p=P))
+
+        nc.sync.dma_start(out=xr[0, 0][:, 0, :], in_=xv[0, :, 0, :])
+        nc.sync.dma_start(out=xr[0, 0][:, 1, :], in_=xv[0, :, 1, :])
+        ws_i = wscale[:].bitcast(I32)
+        for q in range(4):
+            nc.scalar.dma_start(
+                out=ws_i[32 * q : 32 * q + 4, C * D // 4 :].rearrange("p (c n) -> p c n", c=C),
+                in_=beta_scales[:, 4 * q : 4 * q + 4, :].bitcast(I32).rearrange("c q n -> q c n"),
+            )
+        for c in range(C):
+            nc.sync.dma_start(out=bw[:, c, :].bitcast(I32), in_=bv[c])
+        nc.sync.dma_start(out=xr[0, 1][:, 0, :], in_=xv[0, :, 2, :])
+        nc.sync.dma_start(out=xr[0, 1][:, 1, :], in_=xv[0, :, 3, :])
+        for q in range(4):
+            nc.scalar.dma_start(
+                out=ws_i[32 * q : 32 * q + 4, 0 : C * D // 4].rearrange("p (c n) -> p c n", c=C),
+                in_=p_scales[:, 4 * q : 4 * q + 4, :].bitcast(I32).rearrange("c q n -> q c n"),
+            )
+        for h in range(2):
+            for c in range(C):
+                cols = slice(512 * h, 512 * h + 512)
+                nc.sync.dma_start(out=pw[:, c, cols].bitcast(I32), in_=pv[c][:, cols])
+        for g in range(1, G):
+            for h in range(2):
+                nc.sync.dma_start(out=xr[g, h][:], in_=xv[g, :, 2 * h : 2 * h + 2, :])
+            if g == 2:
+                nc.sync.dma_start(out=v_sb[:], in_=v.rearrange("(m p) k -> p m k", p=P))
+
+        banks = {}
+        grouped = {}
+        xcodes = {}
+        xscale = {}
+        ucodes = {}
+        uscale = {}
+        planes_t = {}
+        inter = {}
+
+        def turn(g, tt):
+            bank = tr_pool.tile([P, 4, P], F32, name="trb", tag="trb")
+            banks[g, tt] = bank
+            words = xr[g, tt // 2][:, tt % 2, :].bitcast(F32)
+            for c in range(C):
+                for u in range(2):
+                    nc.tensor.transpose(bank[:, 2 * c + u, :], words[:, 256 * c + u : 256 * (c + 1) : 2], ident[:])
+
+        def xcopy(eng, g, tt):
+            h = tt // 2
+            if (g, h) not in grouped:
+                grouped[g, h] = work.tile([P, 2, C, P, 4], BF16, name="xg", tag="xg", align_bytes=256)
+            dst = grouped[g, h][:, tt % 2].rearrange("p c r e -> p (c r e)").bitcast(F32).rearrange("p (c r u) -> p c r u", c=C, u=2)
+            srcb = banks[g, tt][:].rearrange("p (c u) r -> p c r u", u=2)
+            if eng == "v":
+                nc.vector.tensor_copy(out=dst, in_=srcb)
+            else:
+                nc.scalar.copy(out=dst, in_=srcb)
+
+        def xquant(g, h, parts):
+            if (g, h) not in xcodes:
+                xcodes[g, h] = kept("xc%d%d" % (g, h), [P, 2 * C * P], U32)
+                xscale[g, h] = kept("xs%d%d" % (g, h), [P, 2 * C * P], U8)
+            w = 2 * C * P // 2
+            lo, hi = parts[0] * w, (parts[-1] + 1) * w
+            flat = grouped[g, h][:].rearrange("p t c r e -> p (t c r e)")
+            nc.vector.quantize_mx(
+                out=xcodes[g, h][:, lo:hi].bitcast(FP8X4), scales=xscale[g, h][:, lo:hi], in_=flat[:, 4 * lo : 4 * hi]
+            )
+
+        def mm1(g, n, tt):
+            bank = acc_pool.tile([P, 512], F32, name="acc", tag="acc")
+            banks[g, n, tt] = bank
+            for c in range(C):
+                lo = ((tt % 2) * C + c) * P
+                if n == 0:
+                    rhs = bw[:, c, :]
+                    rs = wscale[:, C * D + c * K : C * D + (c + 1) * K]
+                else:
+                    rhs = pw[:, c, 512 * (n - 1) : 512 * n]
+                    rs = wscale[:, c * D + 512 * (n - 1) : c * D + 512 * n]
+                nc.tensor.matmul_mx(
+                    out=bank[:],
+                    lhsT=xcodes[g, tt // 2][:, lo : lo + P].bitcast(FP8X4),
+                    lhsT_scale=xscale[g, tt // 2][:, lo : lo + P],
+                    rhs=rhs.bitcast(FP8X4),
+                    rhs_scale=rs,
+                    start=(c == 0),
+                    stop=(c == C - 1),
+                )
+
+        def evac(eng, g, n, tt):
+            if (g, n) not in planes_t:
+                planes_t[g, n] = work.tile([P, 4, 512], BF16, name="tb", tag="tb", align_bytes=256)
+            dst = planes_t[g, n][:, tt, :]
+            fac = rt[:, 1 if n == 0 else 0, 4 * g + tt : 4 * g + tt + 1]
+            if eng == "v":
+                nc.vector.tensor_scalar(out=dst, in0=banks[g, n, tt][:], scalar1=fac, scalar2=None, op0=MULT)
+            else:
+                nc.scalar.activation(out=dst, in_=banks[g, n, tt][:], func=COPY, scale=fac)
+
+        def interleave(g, n):
+            inter[g, n] = work.tile([P, 512, 4], BF16, name="il", tag="il", align_bytes=256)
+            nc.vector.tensor_copy(out=inter[g, n][:], in_=planes_t[g, n][:].rearrange("p t n -> p n t"))
+
+        def uquant(g, n):
+            ucodes[g, n] = kept("uc%d%d" % (g, n), [P, 512], U32)
+            uscale[g, n] = kept("us%d%d" % (g, n), [P, 512], U8)
+            nc.vector.quantize_mx(
+                out=ucodes[g, n][:].bitcast(FP8X4), scales=uscale[g, n][:], in_=inter[g, n][:].rearrange("p n t -> p (n t)")
+            )
+
+        def mm2(m, gs):
+            if ("c", m) not in banks:
+                banks["c", m] = acc_pool.tile([P, 512], F32, name="acc", tag="acc")
+            n = 1 + m // 4
+            lo = P * (m % 4)
+            for g in gs:
+                nc.tensor.matmul_mx(
+                    out=banks["c", m][:],
+                    lhsT=ucodes[g, n][:, lo : lo + P].bitcast(FP8X4),
+                    lhsT_scale=uscale[g, n][:, lo : lo + P],
+                    rhs=ucodes[g, 0][:].bitcast(FP8X4),
+                    rhs_scale=uscale[g, 0][:],
+                    start=(g == 0),
+                    stop=(g == G - 1),
+                )
+
+        res = {}
+        resb = {}
+        rgroup = {}
+
+        def finish(m):
+            res[m] = work.tile([P, K], F32, name="res", tag="res", bufs=4, align_bytes=256)
+            nc.vector.scalar_tensor_tensor(
+                out=res[m][:], in0=banks["c", m][:], scalar=rpsi_n[:, m : m + 1], in1=vp[:, m, :], op0=MULT, op1=SUB
+            )
+            nc.sync.dma_start(out=out[P * m : P * m + P, :], in_=res[m][:])
+
+        def roundr(m):
+            resb[m] = work.tile([P, 2, P, 2], BF16, name="resb", tag="resb", align_bytes=256)
+            nc.scalar.copy(out=resb[m][:], in_=res[m][:].rearrange("p (k u e) -> p u k e", u=2, e=2))
+
+        def turnr(m):
+            bank = tr_pool.tile([P, 2, P], F32, name="trb", tag="trb")
+            banks["r", m] = bank
+            words = resb[m][:].rearrange("p u k e -> p (u k e)").bitcast(F32)
+            for u in range(2):
+                nc.tensor.transpose(bank[:, u, :], words[:, P * u : P * u + P], ident[:])
+
+        def rcopy(m):
+            rgroup[m] = work.tile([P, P, 4], BF16, name="rg", tag="rg", align_bytes=256)
+            dst = rgroup[m][:].rearrange("p d e -> p (d e)").bitcast(F32).rearrange("p (d u) -> p d u", u=2)
+            nc.scalar.copy(out=dst, in_=banks["r", m][:].rearrange("p u d -> p d u"))
+
+        def rquant(m):
+            cols = slice(P * m, P * m + P)
+            nc.vector.quantize_mx(
+                out=pcodes[:, cols].bitcast(FP8X4), scales=pscale[:, cols], in_=rgroup[m][:].rearrange("p d e -> p (d e)")
+            )
+
+        ow = out_words.rearrange("g p m t -> (g p) (m t)").bitcast(I32)
+        os_ = out_scales.rearrange("g q m -> (g q) m").bitcast(I32)
+
+        def store_words(m0, m1):
+            nc.sync.dma_start(out=ow[:, P * m0 : P * m1], in_=pcodes[:, P * m0 : P * m1].bitcast(I32))
+
+        def store_scales(m0, m1, engs):
+            for q in range(4):
+                engs[q].dma_start(
+                    out=os_[4 * q : 4 * q + 4, 32 * m0 : 32 * m1],
+                    in_=pscale[32 * q : 32 * q + 4, P * m0 : P * m1].bitcast(I32),
+                )
+
+        turn(0, 0)
+        turn(0, 1)
+        xcopy("s", 0, 0)
+        xcopy("v", 0, 1)
+        xquant(0, 0, [0])
+        xquant(0, 0, [1])
+        nc.vector.tensor_copy(out=rt[:], in_=rt_bf[:])
+        nc.vector.tensor_copy(out=ident_bf[:], in_=ident[:])
+        mm1(0, 0, 0)
+        turn(0, 2)
+        xcopy("s", 0, 2)
+        mm1(0, 0, 1)
+        turn(0, 3)
+        xcopy("v", 0, 3)
+        xquant(0, 1, [0])
+        xquant(0, 1, [1])
+        for tt in range(2):
+            evac("s", 0, 0, tt)
+        for tt in range(2, 4):
+            mm1(0, 0, tt)
+            evac("s", 0, 0, tt)
+
+        for g in range(G):
+            if g:
+                for tt in range(4):
+                    mm1(g, 0, tt)
+                    evac("s", g, 0, tt)
+            interleave(g, 0)
+            if g + 1 < G:
+                turn(g + 1, 0)
+                turn(g + 1, 1)
+                xcopy("v", g + 1, 0)
+                xcopy("s", g + 1, 1)
+            uquant(g, 0)
+            if g + 1 < G:
+                xquant(g + 1, 0, [0, 1])
+            for tt in range(4):
+                mm1(g, 1, tt)
+                evac("s", g, 1, tt)
+            interleave(g, 1)
+            if g + 1 < G:
+                turn(g + 1, 2)
+                turn(g + 1, 3)
+                xcopy("v", g + 1, 2)
+                xcopy("s", g + 1, 3)
+            uquant(g, 1)
+            if g + 1 < G:
+                xquant(g + 1, 1, [0, 1])
+            for tt in range(4):
+                mm1(g, 2, tt)
+                evac("s", g, 2, tt)
+            interleave(g, 2)
+            if g == 0:
+                psi_t = tr_pool.tile([P, P], BF16, name="trb", tag="trb")
+                nc.tensor.transpose(psi_t[:], psi_sb[:], ident_bf[:])
+                nc.vector.reciprocal(out=rpsi[:], in_=psi_t[:, 0:MT])
+            uquant(g, 2)
+            if g == 0:
+                nc.vector.tensor_scalar(out=rpsi_n[:], in0=rpsi[:], scalar1=1.0 / N, scalar2=None, op0=MULT)
+                for m in range(MT):
+                    nc.gpsimd.tensor_scalar(
+                        out=vp[:, m, :], in0=v_sb[:, m, :], scalar1=rpsi[:, m : m + 1], scalar2=0.0, op0=MULT, op1=ADD
+                    )
+
+        for m in range(3):
+            mm2(m, range(G - 1))
+        for m in range(3):
+            mm2(m, [G - 1])
+            finish(m)
+            roundr(m)
+        for m in range(3, MT):
+            turnr(m - 3)
+            rcopy(m - 3)
+            mm2(m, range(G))
+            rquant(m - 3)
+            finish(m)
+            roundr(m)
+            if m == 5:
+                store_words(0, 2)
+            if m == 7:
+                store_words(2, 4)
+        store_scales(0, 4, [nc.sync] * 4)
+        for m in range(MT - 3, MT):
+            turnr(m)
+            rcopy(m)
+            rquant(m)
+            if m == 5:
+                store_words(4, 6)
+        store_words(6, 8)
+        store_scales(4, 8, [nc.sync, nc.scalar, nc.sync, nc.scalar])

@@ -40,15 +40,12 @@ def tile_factoranalysisemloadinggradient_x2_kernel(
         ident = kept("ident", [P, P], F32)
         ident_bf = kept("ident_bf", [P, P], BF16)
         wscale = kept("wscale", [P, C * (D + K)], U8)
-        psi_sb = kept("psi_sb", [P, P], BF16)
-        rt_bf = kept("rt_bf", [P, 2, 16], BF16)
-        rt = kept("rt", [P, 2, 16], F32)
+        vec = kept("vec", [P, 512], BF16)
+        rt = kept("rt", [P, 4, 2 * G], F32)
         pw = kept("pw", [P, C, D], U32)
         bw = kept("bw", [P, C, K], U32)
         rpsi = kept("rpsi", [P, MT], F32)
-        rpsi_n = kept("rpsi_n", [P, MT], F32)
         v_sb = kept("v_sb", [P, MT, K], BF16)
-        vp = kept("vp", [P, MT, K], F32)
         pcodes = kept("pcodes", [P, D], U32)
         pscale = kept("pscale", [P, D], U8)
 
@@ -63,11 +60,11 @@ def tile_factoranalysisemloadinggradient_x2_kernel(
 
         nc.gpsimd.memset(wscale[:].bitcast(I32), 0)
         make_identity(nc, ident[:])
-        nc.gpsimd.dma_start(out=rt_bf[:, 0, :].rearrange("p (g t) -> p g t", t=4), in_=r.rearrange("(g p t) -> p g t", g=G, t=4))
-        nc.gpsimd.dma_start(out=rt_bf[:, 1, :].rearrange("p (g t) -> p g t", t=4), in_=t.rearrange("(g p t) -> p g t", g=G, t=4))
-        nc.gpsimd.memset(psi_sb[:], 0.0)
-        nc.gpsimd.dma_start(out=psi_sb[0:MT, :], in_=psi.rearrange("(m p) -> m p", p=P))
-
+        nc.vector.memset(vec[:].bitcast(I32), 0)
+        nc.vector.tensor_copy(out=ident_bf[:], in_=ident[:])
+        nc.scalar.dma_start(out=vec[0:G, :], in_=r.rearrange("(g n) -> g n", g=G))
+        nc.scalar.dma_start(out=vec[G : 2 * G, :], in_=t.rearrange("(g n) -> g n", g=G))
+        nc.scalar.dma_start(out=vec[2 * G : 2 * G + MT, 0:P], in_=psi.rearrange("(m p) -> m p", p=P))
         nc.sync.dma_start(out=xr[0, 0][:, 0, :], in_=xv[0, :, 0, :])
         nc.sync.dma_start(out=xr[0, 0][:, 1, :], in_=xv[0, :, 1, :])
         ws_i = wscale[:].bitcast(I32)
@@ -76,9 +73,9 @@ def tile_factoranalysisemloadinggradient_x2_kernel(
                 out=ws_i[32 * q : 32 * q + 4, C * D // 4 :].rearrange("p (c n) -> p c n", c=C),
                 in_=beta_scales[:, 4 * q : 4 * q + 4, :].bitcast(I32).rearrange("c q n -> q c n"),
             )
+        nc.sync.dma_start(out=xr[0, 1][:, 0, :], in_=xv[0, :, 2, :])
         for c in range(C):
             nc.sync.dma_start(out=bw[:, c, :].bitcast(I32), in_=bv[c])
-        nc.sync.dma_start(out=xr[0, 1][:, 0, :], in_=xv[0, :, 2, :])
         nc.sync.dma_start(out=xr[0, 1][:, 1, :], in_=xv[0, :, 3, :])
         for q in range(4):
             nc.scalar.dma_start(
@@ -104,13 +101,31 @@ def tile_factoranalysisemloadinggradient_x2_kernel(
         planes_t = {}
         inter = {}
 
+        sorted_x = {}
+
+        def sortx(eng, g, h):
+            sorted_x[g, h] = work.tile([P, 2, C, 2, P], F32, name="sx", tag="sx", align_bytes=256)
+            srcw = xr[g, h][:].rearrange("p t k -> p (t k)").bitcast(F32).rearrange("p (b w u) -> p b u w", b=2 * C, u=2)
+            dst = sorted_x[g, h][:].rearrange("p t c u w -> p (t c) u w")
+            if eng == "v":
+                nc.vector.tensor_copy(out=dst, in_=srcw)
+            else:
+                nc.scalar.copy(out=dst, in_=srcw)
+
         def turn(g, tt):
-            bank = tr_pool.tile([P, 4, P], F32, name="trb", tag="trb")
+            if g == 0:
+                bank = acc_pool.tile([P, 4, P], F32, name="acc", tag="acc")
+            else:
+                bank = tr_pool.tile([P, 4, P], F32, name="trb", tag="trb")
             banks[g, tt] = bank
             words = xr[g, tt // 2][:, tt % 2, :].bitcast(F32)
             for c in range(C):
                 for u in range(2):
-                    nc.tensor.transpose(bank[:, 2 * c + u, :], words[:, 256 * c + u : 256 * (c + 1) : 2], ident[:])
+                    if (g, tt // 2) in sorted_x:
+                        src = sorted_x[g, tt // 2][:, tt % 2, c, u, :]
+                    else:
+                        src = words[:, 256 * c + u : 256 * (c + 1) : 2]
+                    nc.tensor.transpose(bank[:, 2 * c + u, :], src, ident[:])
 
         def xcopy(eng, g, tt):
             h = tt // 2
@@ -159,7 +174,8 @@ def tile_factoranalysisemloadinggradient_x2_kernel(
             if (g, n) not in planes_t:
                 planes_t[g, n] = work.tile([P, 4, 512], BF16, name="tb", tag="tb", align_bytes=256)
             dst = planes_t[g, n][:, tt, :]
-            fac = rt[:, 1 if n == 0 else 0, 4 * g + tt : 4 * g + tt + 1]
+            col = (G if n == 0 else 0) + g
+            fac = rt[:, tt, col : col + 1]
             if eng == "v":
                 nc.vector.tensor_scalar(out=dst, in0=banks[g, n, tt][:], scalar1=fac, scalar2=None, op0=MULT)
             else:
@@ -196,33 +212,53 @@ def tile_factoranalysisemloadinggradient_x2_kernel(
         resb = {}
         rgroup = {}
 
+        diff = {}
+
+        def subtract(m):
+            diff[m] = work.tile([P, K], F32, name="diff", tag="diff", bufs=4, align_bytes=256)
+            nc.vector.scalar_tensor_tensor(
+                out=diff[m][:], in0=banks["c", m][:], scalar=1.0 / N, in1=v_sb[:, m, :], op0=MULT, op1=SUB
+            )
+
         def finish(m):
             res[m] = work.tile([P, K], F32, name="res", tag="res", bufs=4, align_bytes=256)
-            nc.vector.scalar_tensor_tensor(
-                out=res[m][:], in0=banks["c", m][:], scalar=rpsi_n[:, m : m + 1], in1=vp[:, m, :], op0=MULT, op1=SUB
-            )
+            nc.scalar.activation(out=res[m][:], in_=diff[m][:], func=COPY, scale=rpsi[:, m : m + 1])
             nc.sync.dma_start(out=out[P * m : P * m + P, :], in_=res[m][:])
 
         def roundr(m):
-            resb[m] = work.tile([P, 2, P, 2], BF16, name="resb", tag="resb", align_bytes=256)
-            nc.scalar.copy(out=resb[m][:], in_=res[m][:].rearrange("p (k u e) -> p u k e", u=2, e=2))
+            resb[m] = work.tile([P, 2, P, 2], BF16, name="resb", tag="resb", bufs=3, align_bytes=256)
+            nc.vector.tensor_scalar(
+                out=resb[m][:],
+                in0=diff[m][:].rearrange("p (k u e) -> p u k e", u=2, e=2),
+                scalar1=rpsi[:, m : m + 1],
+                scalar2=None,
+                op0=MULT,
+            )
 
-        def turnr(m):
-            bank = tr_pool.tile([P, 2, P], F32, name="trb", tag="trb")
-            banks["r", m] = bank
-            words = resb[m][:].rearrange("p u k e -> p (u k e)").bitcast(F32)
-            for u in range(2):
-                nc.tensor.transpose(bank[:, u, :], words[:, P * u : P * u + P], ident[:])
+        def turnr(ms):
+            bank = tr_pool.tile([P, len(ms), 2, P], F32, name="trb", tag="trb")
+            banks["r", ms[0]] = bank
+            for i, m in enumerate(ms):
+                words = resb[m][:].rearrange("p u k e -> p (u k e)").bitcast(F32)
+                for u in range(2):
+                    nc.tensor.transpose(bank[:, i, u, :], words[:, P * u : P * u + P], ident[:])
 
-        def rcopy(m):
-            rgroup[m] = work.tile([P, P, 4], BF16, name="rg", tag="rg", align_bytes=256)
-            dst = rgroup[m][:].rearrange("p d e -> p (d e)").bitcast(F32).rearrange("p (d u) -> p d u", u=2)
-            nc.scalar.copy(out=dst, in_=banks["r", m][:].rearrange("p u d -> p d u"))
+        def rcopy(ms, eng="s"):
+            rgroup[ms[0]] = work.tile([P, len(ms) * P, 4], BF16, name="rg", tag="rg", align_bytes=256)
+            dst = (
+                rgroup[ms[0]][:].rearrange("p d e -> p (d e)").bitcast(F32)
+                .rearrange("p (i d u) -> p i d u", i=len(ms), u=2)
+            )
+            srcb = banks["r", ms[0]][:].rearrange("p i u d -> p i d u")
+            if eng == "v":
+                nc.vector.tensor_copy(out=dst, in_=srcb)
+            else:
+                nc.scalar.copy(out=dst, in_=srcb)
 
-        def rquant(m):
-            cols = slice(P * m, P * m + P)
+        def rquant(ms):
+            cols = slice(P * ms[0], P * ms[-1] + P)
             nc.vector.quantize_mx(
-                out=pcodes[:, cols].bitcast(FP8X4), scales=pscale[:, cols], in_=rgroup[m][:].rearrange("p d e -> p (d e)")
+                out=pcodes[:, cols].bitcast(FP8X4), scales=pscale[:, cols], in_=rgroup[ms[0]][:].rearrange("p d e -> p (d e)")
             )
 
         ow = out_words.rearrange("g p m t -> (g p) (m t)").bitcast(I32)
@@ -240,25 +276,31 @@ def tile_factoranalysisemloadinggradient_x2_kernel(
 
         turn(0, 0)
         turn(0, 1)
+        vt = tr_pool.tile([P, 4, P], BF16, name="trb", tag="trb")
+        for tt in range(4):
+            nc.tensor.transpose(vt[:, tt, :], vec[:, tt:512:4], ident_bf[:])
+        psi_t = tr_pool.tile([P, P], BF16, name="trb", tag="trb")
+        nc.tensor.transpose(psi_t[:], vec[:, 0:P], ident_bf[:])
         xcopy("s", 0, 0)
         xcopy("v", 0, 1)
         xquant(0, 0, [0])
+        nc.vector.tensor_copy(out=rt[:], in_=vt[:, :, 0 : 2 * G])
         xquant(0, 0, [1])
-        nc.vector.tensor_copy(out=rt[:], in_=rt_bf[:])
-        nc.vector.tensor_copy(out=ident_bf[:], in_=ident[:])
-        mm1(0, 0, 0)
+        nc.vector.reciprocal(out=rpsi[:], in_=psi_t[:, 2 * G : 2 * G + MT])
         turn(0, 2)
         xcopy("s", 0, 2)
-        mm1(0, 0, 1)
+        mm1(0, 0, 0)
         turn(0, 3)
         xcopy("v", 0, 3)
         xquant(0, 1, [0])
         xquant(0, 1, [1])
+        mm1(0, 0, 1)
         for tt in range(2):
             evac("s", 0, 0, tt)
         for tt in range(2, 4):
             mm1(0, 0, tt)
             evac("s", 0, 0, tt)
+        sortx("v", 1, 0)
 
         for g in range(G):
             if g:
@@ -267,64 +309,81 @@ def tile_factoranalysisemloadinggradient_x2_kernel(
                     evac("s", g, 0, tt)
             interleave(g, 0)
             if g + 1 < G:
+                sortx("v", g + 1, 1)
                 turn(g + 1, 0)
                 turn(g + 1, 1)
-                xcopy("v", g + 1, 0)
+                xcopy("s", g + 1, 0)
                 xcopy("s", g + 1, 1)
             uquant(g, 0)
-            if g + 1 < G:
-                xquant(g + 1, 0, [0, 1])
             for tt in range(4):
                 mm1(g, 1, tt)
                 evac("s", g, 1, tt)
+            if g + 1 < G:
+                xquant(g + 1, 0, [0, 1])
             interleave(g, 1)
             if g + 1 < G:
                 turn(g + 1, 2)
                 turn(g + 1, 3)
-                xcopy("v", g + 1, 2)
+                xcopy("s", g + 1, 2)
                 xcopy("s", g + 1, 3)
+            if g + 2 < G:
+                sortx("v", g + 2, 0)
             uquant(g, 1)
-            if g + 1 < G:
-                xquant(g + 1, 1, [0, 1])
             for tt in range(4):
                 mm1(g, 2, tt)
                 evac("s", g, 2, tt)
+            if g + 1 < G:
+                xquant(g + 1, 1, [0, 1])
             interleave(g, 2)
-            if g == 0:
-                psi_t = tr_pool.tile([P, P], BF16, name="trb", tag="trb")
-                nc.tensor.transpose(psi_t[:], psi_sb[:], ident_bf[:])
-                nc.vector.reciprocal(out=rpsi[:], in_=psi_t[:, 0:MT])
             uquant(g, 2)
-            if g == 0:
-                nc.vector.tensor_scalar(out=rpsi_n[:], in0=rpsi[:], scalar1=1.0 / N, scalar2=None, op0=MULT)
-                for m in range(MT):
-                    nc.gpsimd.tensor_scalar(
-                        out=vp[:, m, :], in0=v_sb[:, m, :], scalar1=rpsi[:, m : m + 1], scalar2=0.0, op0=MULT, op1=ADD
-                    )
 
         for m in range(3):
             mm2(m, range(G - 1))
         for m in range(3):
             mm2(m, [G - 1])
+            subtract(m)
             finish(m)
-            roundr(m)
-        for m in range(3, MT):
-            turnr(m - 3)
-            rcopy(m - 3)
-            mm2(m, range(G))
-            rquant(m - 3)
-            finish(m)
-            roundr(m)
-            if m == 5:
-                store_words(0, 2)
-            if m == 7:
-                store_words(2, 4)
+        mm2(3, range(G))
+        roundr(0)
+        roundr(1)
+        subtract(3)
+        finish(3)
+        mm2(4, range(G))
+        turnr([0, 1])
+        roundr(2)
+        rcopy([0, 1])
+        subtract(4)
+        roundr(3)
+        finish(4)
+        mm2(5, range(G))
+        rquant([0, 1])
+        store_words(0, 2)
+        turnr([2, 3])
+        rcopy([2, 3])
+        roundr(4)
+        subtract(5)
+        finish(5)
+        roundr(5)
+        rquant([2, 3])
+        store_words(2, 4)
         store_scales(0, 4, [nc.sync] * 4)
-        for m in range(MT - 3, MT):
-            turnr(m)
-            rcopy(m)
-            rquant(m)
-            if m == 5:
-                store_words(4, 6)
+        mm2(6, range(G))
+        turnr([4, 5])
+        rcopy([4, 5])
+        subtract(6)
+        mm2(7, range(G))
+        rquant([4, 5])
+        store_words(4, 6)
+        roundr(6)
+        finish(6)
+        turnr([6])
+        subtract(7)
+        rcopy([6])
+        roundr(7)
+        turnr([7])
+        rquant([6])
+        rcopy([7], "v")
+        finish(7)
+        rquant([7])
         store_words(6, 8)
         store_scales(4, 8, [nc.sync, nc.scalar, nc.sync, nc.scalar])

@@ -41,6 +41,7 @@ def tile_factoranalysisemloadinggradient_x2_kernel(
         ident_bf = kept("ident_bf", [P, P], BF16)
         wscale = kept("wscale", [P, C * (D + K)], U8)
         vec = kept("vec", [P, 512], BF16)
+        psi_sb = kept("psi_sb", [P, P], BF16)
         rt = kept("rt", [P, 4, 2 * G], F32)
         pw = kept("pw", [P, C, D], U32)
         bw = kept("bw", [P, C, K], U32)
@@ -58,39 +59,39 @@ def tile_factoranalysisemloadinggradient_x2_kernel(
             for h in range(2):
                 xr[g, h] = kept("xr%d%d" % (g, h), [P, 2, D], BF16)
 
-        nc.gpsimd.memset(wscale[:].bitcast(I32), 0)
-        make_identity(nc, ident[:])
+        ws_i = wscale[:].bitcast(I32)
+
+        def load_scales(eng, src, lo, width):
+            for q in range(4):
+                eng.dma_start(
+                    out=ws_i[32 * q : 32 * q + 4, lo // 4 : (lo + C * width) // 4].rearrange("p (c n) -> p c n", c=C),
+                    in_=src[:, 4 * q : 4 * q + 4, :].bitcast(I32).rearrange("c q n -> q c n"),
+                )
+
+        def load_p(h):
+            cols = slice(512 * h, 512 * h + 512)
+            nc.sync.dma_start(out=pw[:, :, cols].bitcast(I32), in_=pv.rearrange("c p n -> p c n")[:, :, cols])
+
+        nc.vector.memset(ws_i, 0)
         nc.vector.memset(vec[:].bitcast(I32), 0)
+        nc.gpsimd.dma_start(out=bw[:].bitcast(I32), in_=bv.rearrange("c p n -> p c n"))
+        make_identity(nc, ident[:])
         nc.vector.tensor_copy(out=ident_bf[:], in_=ident[:])
-        nc.scalar.dma_start(out=vec[0:G, :], in_=r.rearrange("(g n) -> g n", g=G))
-        nc.scalar.dma_start(out=vec[G : 2 * G, :], in_=t.rearrange("(g n) -> g n", g=G))
-        nc.scalar.dma_start(out=vec[2 * G : 2 * G + MT, 0:P], in_=psi.rearrange("(m p) -> m p", p=P))
+        nc.vector.memset(psi_sb[:].bitcast(I32), 0)
         nc.sync.dma_start(out=xr[0, 0][:, 0, :], in_=xv[0, :, 0, :])
         nc.sync.dma_start(out=xr[0, 0][:, 1, :], in_=xv[0, :, 1, :])
-        ws_i = wscale[:].bitcast(I32)
-        for q in range(4):
-            nc.scalar.dma_start(
-                out=ws_i[32 * q : 32 * q + 4, C * D // 4 :].rearrange("p (c n) -> p c n", c=C),
-                in_=beta_scales[:, 4 * q : 4 * q + 4, :].bitcast(I32).rearrange("c q n -> q c n"),
-            )
-        nc.sync.dma_start(out=xr[0, 1][:, 0, :], in_=xv[0, :, 2, :])
-        for c in range(C):
-            nc.sync.dma_start(out=bw[:, c, :].bitcast(I32), in_=bv[c])
-        nc.sync.dma_start(out=xr[0, 1][:, 1, :], in_=xv[0, :, 3, :])
-        for q in range(4):
-            nc.scalar.dma_start(
-                out=ws_i[32 * q : 32 * q + 4, 0 : C * D // 4].rearrange("p (c n) -> p c n", c=C),
-                in_=p_scales[:, 4 * q : 4 * q + 4, :].bitcast(I32).rearrange("c q n -> q c n"),
-            )
-        for h in range(2):
-            for c in range(C):
-                cols = slice(512 * h, 512 * h + 512)
-                nc.sync.dma_start(out=pw[:, c, cols].bitcast(I32), in_=pv[c][:, cols])
+        load_scales(nc.sync, beta_scales, C * D, K)
+        nc.sync.dma_start(out=xr[0, 1][:], in_=xv[0, :, 2:4, :])
+        nc.sync.dma_start(out=vec[G : 2 * G, :], in_=t.rearrange("(g n) -> g n", g=G))
+        nc.sync.dma_start(out=vec[0:G, :], in_=r.rearrange("(g n) -> g n", g=G))
+        load_scales(nc.sync, p_scales, 0, D)
+        load_p(0)
+        load_p(1)
         for g in range(1, G):
             for h in range(2):
                 nc.sync.dma_start(out=xr[g, h][:], in_=xv[g, :, 2 * h : 2 * h + 2, :])
-            if g == 2:
-                nc.sync.dma_start(out=v_sb[:], in_=v.rearrange("(m p) k -> p m k", p=P))
+        nc.sync.dma_start(out=psi_sb[0:MT, :], in_=psi.rearrange("(m p) -> m p", p=P))
+        nc.sync.dma_start(out=v_sb[:], in_=v.rearrange("(m p) k -> p m k", p=P))
 
         banks = {}
         grouped = {}
@@ -183,7 +184,10 @@ def tile_factoranalysisemloadinggradient_x2_kernel(
 
         def interleave(g, n):
             inter[g, n] = work.tile([P, 512, 4], BF16, name="il", tag="il", align_bytes=256)
-            nc.vector.tensor_copy(out=inter[g, n][:], in_=planes_t[g, n][:].rearrange("p t n -> p n t"))
+            nc.vector.tensor_copy(
+                out=inter[g, n][:].rearrange("p (c i) t -> p c t i", i=4),
+                in_=planes_t[g, n][:].rearrange("p t (c i) -> p c t i", i=4),
+            )
 
         def uquant(g, n):
             ucodes[g, n] = kept("uc%d%d" % (g, n), [P, 512], U32)
@@ -276,65 +280,76 @@ def tile_factoranalysisemloadinggradient_x2_kernel(
 
         turn(0, 0)
         turn(0, 1)
-        vt = tr_pool.tile([P, 4, P], BF16, name="trb", tag="trb")
-        for tt in range(4):
-            nc.tensor.transpose(vt[:, tt, :], vec[:, tt:512:4], ident_bf[:])
-        psi_t = tr_pool.tile([P, P], BF16, name="trb", tag="trb")
-        nc.tensor.transpose(psi_t[:], vec[:, 0:P], ident_bf[:])
+        turn(0, 2)
+        turn(0, 3)
         xcopy("s", 0, 0)
         xcopy("v", 0, 1)
         xquant(0, 0, [0])
-        nc.vector.tensor_copy(out=rt[:], in_=vt[:, :, 0 : 2 * G])
-        xquant(0, 0, [1])
-        nc.vector.reciprocal(out=rpsi[:], in_=psi_t[:, 2 * G : 2 * G + MT])
-        turn(0, 2)
         xcopy("s", 0, 2)
-        mm1(0, 0, 0)
-        turn(0, 3)
+        xquant(0, 0, [1])
         xcopy("v", 0, 3)
+        mm1(0, 0, 0)
+        vt = tr_pool.tile([P, 4, P], BF16, name="trb", tag="trb")
+        for tt in range(4):
+            nc.tensor.transpose(vt[:, tt, :], vec[:, tt:512:4], ident_bf[:])
         xquant(0, 1, [0])
+        nc.vector.tensor_copy(out=rt[:], in_=vt[:, :, 0 : 2 * G])
         xquant(0, 1, [1])
-        mm1(0, 0, 1)
-        for tt in range(2):
-            evac("s", 0, 0, tt)
-        for tt in range(2, 4):
+        evac("s", 0, 0, 0)
+        for tt in range(1, 4):
             mm1(0, 0, tt)
             evac("s", 0, 0, tt)
-        sortx("v", 1, 0)
 
-        for g in range(G):
-            if g:
-                for tt in range(4):
-                    mm1(g, 0, tt)
-                    evac("s", g, 0, tt)
-            interleave(g, 0)
+        def turn_half(g, h, engs="ss"):
+            turn(g, 2 * h)
+            turn(g, 2 * h + 1)
+            xcopy(engs[0], g, 2 * h)
+            xcopy(engs[1], g, 2 * h + 1)
+
+        def unit(g, n, tts=range(4)):
+            for tt in tts:
+                mm1(g, n, tt)
+                evac("s", g, n, tt)
+
+        sortx("v", 1, 0)
+        unit(0, 1)
+        interleave(0, 0)
+        turn_half(1, 0)
+        sortx("v", 1, 1)
+        uquant(0, 0)
+        unit(0, 2, range(2))
+        interleave(0, 1)
+        turn_half(1, 1)
+        unit(0, 2, range(2, 4))
+        xquant(1, 0, [0, 1])
+        uquant(0, 1)
+        xquant(1, 1, [0, 1])
+        sortx("v", 2, 0)
+        interleave(0, 2)
+        uquant(0, 2)
+        for g in range(1, G):
+            unit(g, 0)
             if g + 1 < G:
                 sortx("v", g + 1, 1)
-                turn(g + 1, 0)
-                turn(g + 1, 1)
-                xcopy("s", g + 1, 0)
-                xcopy("s", g + 1, 1)
+                turn_half(g + 1, 0)
+            interleave(g, 0)
+            unit(g, 1)
             uquant(g, 0)
-            for tt in range(4):
-                mm1(g, 1, tt)
-                evac("s", g, 1, tt)
             if g + 1 < G:
+                turn_half(g + 1, 1)
                 xquant(g + 1, 0, [0, 1])
             interleave(g, 1)
-            if g + 1 < G:
-                turn(g + 1, 2)
-                turn(g + 1, 3)
-                xcopy("s", g + 1, 2)
-                xcopy("s", g + 1, 3)
-            if g + 2 < G:
-                sortx("v", g + 2, 0)
-            uquant(g, 1)
-            for tt in range(4):
-                mm1(g, 2, tt)
-                evac("s", g, 2, tt)
+            unit(g, 2)
             if g + 1 < G:
                 xquant(g + 1, 1, [0, 1])
+            uquant(g, 1)
+            if g + 2 < G:
+                sortx("v", g + 2, 0)
             interleave(g, 2)
+            if g == 2:
+                psi_t = tr_pool.tile([P, P], BF16, name="trb", tag="trb")
+                nc.tensor.transpose(psi_t[:], psi_sb[:], ident_bf[:])
+                nc.vector.reciprocal(out=rpsi[:], in_=psi_t[:, 0:MT])
             uquant(g, 2)
 
         for m in range(3):

@@ -21,6 +21,9 @@ P = 128
 G = N // 512
 C = D // 512
 MT = D // P
+XC = {(1,1): "vs", (2,1): "vs", (3,1): "vs"}
+NOSORT = [(1,1), (2,1), (3,1)]
+FUSED = []
 
 
 def tile_factoranalysisemloadinggradient_x2_kernel(
@@ -105,6 +108,8 @@ def tile_factoranalysisemloadinggradient_x2_kernel(
         sorted_x = {}
 
         def sortx(eng, g, h):
+            if (g, h) in NOSORT:
+                return
             sorted_x[g, h] = work.tile([P, 2, C, 2, P], F32, name="sx", tag="sx", align_bytes=256)
             srcw = xr[g, h][:].rearrange("p t k -> p (t k)").bitcast(F32).rearrange("p (b w u) -> p b u w", b=2 * C, u=2)
             dst = sorted_x[g, h][:].rearrange("p t c u w -> p (t c) u w")
@@ -171,6 +176,36 @@ def tile_factoranalysisemloadinggradient_x2_kernel(
                     stop=(c == C - 1),
                 )
 
+        def unit_fused(g, n):
+            inter[g, n] = work.tile([P, 512, 4], BF16, name="il", tag="il", align_bytes=256)
+            col = (G if n == 0 else 0) + g
+            for j in range(4):
+                bank = acc_pool.tile([P, 4, P], F32, name="acc", tag="acc")
+                for tt in range(4):
+                    for c in range(C):
+                        lo = ((tt % 2) * C + c) * P
+                        if n == 0:
+                            rhs = bw[:, c, P * j : P * j + P]
+                            off = C * D + c * K + P * j
+                        else:
+                            rhs = pw[:, c, 512 * (n - 1) + P * j : 512 * (n - 1) + P * j + P]
+                            off = c * D + 512 * (n - 1) + P * j
+                        nc.tensor.matmul_mx(
+                            out=bank[:, tt, :],
+                            lhsT=xcodes[g, tt // 2][:, lo : lo + P].bitcast(FP8X4),
+                            lhsT_scale=xscale[g, tt // 2][:, lo : lo + P],
+                            rhs=rhs.bitcast(FP8X4),
+                            rhs_scale=wscale[:, off : off + P],
+                            start=(c == 0),
+                            stop=(c == C - 1),
+                        )
+                nc.vector.tensor_tensor(
+                    out=inter[g, n][:, P * j : P * j + P, :],
+                    in0=bank[:].rearrange("p t n -> p n t"),
+                    in1=rt[:, :, col : col + 1].rearrange("p t o -> p o t").to_broadcast([P, P, 4]),
+                    op=MULT,
+                )
+
         def evac(eng, g, n, tt):
             if (g, n) not in planes_t:
                 planes_t[g, n] = work.tile([P, 4, 512], BF16, name="tb", tag="tb", align_bytes=256)
@@ -183,6 +218,8 @@ def tile_factoranalysisemloadinggradient_x2_kernel(
                 nc.scalar.activation(out=dst, in_=banks[g, n, tt][:], func=COPY, scale=fac)
 
         def interleave(g, n):
+            if (g, n) in FUSED:
+                return
             inter[g, n] = work.tile([P, 512, 4], BF16, name="il", tag="il", align_bytes=256)
             nc.vector.tensor_copy(
                 out=inter[g, n][:].rearrange("p (c i) t -> p c t i", i=4),
@@ -301,12 +338,16 @@ def tile_factoranalysisemloadinggradient_x2_kernel(
             evac("s", 0, 0, tt)
 
         def turn_half(g, h, engs="ss"):
+            engs = XC.get((g, h), engs)
             turn(g, 2 * h)
             turn(g, 2 * h + 1)
             xcopy(engs[0], g, 2 * h)
             xcopy(engs[1], g, 2 * h + 1)
 
         def unit(g, n, tts=range(4)):
+            if (g, n) in FUSED:
+                unit_fused(g, n)
+                return
             for tt in tts:
                 mm1(g, n, tt)
                 evac("s", g, n, tt)
@@ -386,19 +427,19 @@ def tile_factoranalysisemloadinggradient_x2_kernel(
         turnr([4, 5])
         rcopy([4, 5])
         subtract(6)
-        mm2(7, range(G))
-        rquant([4, 5])
-        store_words(4, 6)
         roundr(6)
         finish(6)
+        mm2(7, range(G))
         turnr([6])
-        subtract(7)
         rcopy([6])
-        roundr(7)
-        turnr([7])
-        rquant([6])
-        rcopy([7], "v")
+        subtract(7)
         finish(7)
+        rquant([4, 5])
+        store_words(4, 6)
+        roundr(7)
+        rquant([6])
+        turnr([7])
+        rcopy([7])
         rquant([7])
         store_words(6, 8)
         store_scales(4, 8, [nc.sync, nc.scalar, nc.sync, nc.scalar])

from contextlib import ExitStack

import concourse.mybir as mybir
from concourse.masks import make_identity

N, D, K = 2048, 1024, 512
FLOPS = 2 * N * D * (D + K) + 2 * N * D * K

F32 = mybir.dt.float32
BF16 = mybir.dt.bfloat16
I32 = mybir.dt.int32
U32 = mybir.dt.uint32
U8 = mybir.dt.uint8
FP8X4 = mybir.dt.float8_e4m3fn_x4
COPY = mybir.ActivationFunctionType.Copy
MULT = mybir.AluOpType.mult
ADD = mybir.AluOpType.add
SUB = mybir.AluOpType.subtract

P = 128
G = N // 512
C = D // 512
MT = D // P
XC = {(1,1): "vs", (2,1): "vs", (3,1): "vs"}
NOSORT = [(1,1), (2,1), (3,1)]
FUSED = []


def tile_factoranalysisemloadinggradient_x2_kernel(
    tc, x, p_words, p_scales, beta_words, beta_scales, r, t, v, psi, out, out_words, out_scales
):
    nc = tc.nc
    with ExitStack() as ctx:
        keep = ctx.enter_context(tc.tile_pool(name="keep", bufs=1))
        work = ctx.enter_context(tc.tile_pool(name="work", bufs=2))
        acc_pool = ctx.enter_context(tc.psum_pool(name="acc", bufs=6))
        tr_pool = ctx.enter_context(tc.psum_pool(name="tr", bufs=2))
        ctx.enter_context(tc.manual_schedule())

        def kept(name, shape, dtype):
            return keep.tile(shape, dtype, name=name, tag=name, align_bytes=256)

        ident = kept("ident", [P, P], F32)
        ident_bf = kept("ident_bf", [P, P], BF16)
        wscale = kept("wscale", [P, C * (D + K)], U8)
        vec = kept("vec", [P, 512], BF16)
        psi_sb = kept("psi_sb", [P, P], BF16)
        rt = kept("rt", [P, 4, 2 * G], F32)
        pw = kept("pw", [P, C, D], U32)
        bw = kept("bw", [P, C, K], U32)
        rpsi = kept("rpsi", [P, MT], F32)
        v_sb = kept("v_sb", [P, MT, K], BF16)
        pcodes = kept("pcodes", [P, D], U32)
        pscale = kept("pscale", [P, D], U8)

        xv = x.rearrange("(g p t) k -> g p t k", g=G, t=4)
        pv = p_words.rearrange("c p n t -> c p (n t)").bitcast(I32)
        bv = beta_words.rearrange("c p n t -> c p (n t)").bitcast(I32)

        xr = {}
        for g in range(G):
            for h in range(2):
                xr[g, h] = kept("xr%d%d" % (g, h), [P, 2, D], BF16)

        ws_i = wscale[:].bitcast(I32)

        def load_scales(eng, src, lo, width):
            for q in range(4):
                eng.dma_start(
                    out=ws_i[32 * q : 32 * q + 4, lo // 4 : (lo + C * width) // 4].rearrange("p (c n) -> p c n", c=C),
                    in_=src[:, 4 * q : 4 * q + 4, :].bitcast(I32).rearrange("c q n -> q c n"),
                )

        def load_p(h):
            cols = slice(512 * h, 512 * h + 512)
            nc.sync.dma_start(out=pw[:, :, cols].bitcast(I32), in_=pv.rearrange("c p n -> p c n")[:, :, cols])

        nc.vector.memset(ws_i, 0)
        nc.vector.memset(vec[:].bitcast(I32), 0)
        nc.gpsimd.dma_start(out=bw[:].bitcast(I32), in_=bv.rearrange("c p n -> p c n"))
        make_identity(nc, ident[:])
        nc.vector.tensor_copy(out=ident_bf[:], in_=ident[:])
        nc.vector.memset(psi_sb[:].bitcast(I32), 0)
        nc.sync.dma_start(out=xr[0, 0][:, 0, :], in_=xv[0, :, 0, :])
        nc.sync.dma_start(out=xr[0, 0][:, 1, :], in_=xv[0, :, 1, :])
        load_scales(nc.sync, beta_scales, C * D, K)
        nc.sync.dma_start(out=xr[0, 1][:], in_=xv[0, :, 2:4, :])
        nc.sync.dma_start(out=vec[G : 2 * G, :], in_=t.rearrange("(g n) -> g n", g=G))
        nc.sync.dma_start(out=vec[0:G, :], in_=r.rearrange("(g n) -> g n", g=G))
        load_scales(nc.sync, p_scales, 0, D)
        load_p(0)
        load_p(1)
        for g in range(1, G):
            for h in range(2):
                nc.sync.dma_start(out=xr[g, h][:], in_=xv[g, :, 2 * h : 2 * h + 2, :])
        nc.sync.dma_start(out=psi_sb[0:MT, :], in_=psi.rearrange("(m p) -> m p", p=P))
        nc.sync.dma_start(out=v_sb[:], in_=v.rearrange("(m p) k -> p m k", p=P))

        banks = {}
        grouped = {}
        xcodes = {}
        xscale = {}
        ucodes = {}
        uscale = {}
        planes_t = {}
        inter = {}

        sorted_x = {}

        def sortx(eng, g, h):
            if (g, h) in NOSORT:
                return
            sorted_x[g, h] = work.tile([P, 2, C, 2, P], F32, name="sx", tag="sx", align_bytes=256)
            srcw = xr[g, h][:].rearrange("p t k -> p (t k)").bitcast(F32).rearrange("p (b w u) -> p b u w", b=2 * C, u=2)
            dst = sorted_x[g, h][:].rearrange("p t c u w -> p (t c) u w")
            if eng == "v":
                nc.vector.tensor_copy(out=dst, in_=srcw)
            else:
                nc.scalar.copy(out=dst, in_=srcw)

        def turn(g, tt):
            if g == 0:
                bank = acc_pool.tile([P, 4, P], F32, name="acc", tag="acc")
            else:
                bank = tr_pool.tile([P, 4, P], F32, name="trb", tag="trb")
            banks[g, tt] = bank
            words = xr[g, tt // 2][:, tt % 2, :].bitcast(F32)
            for c in range(C):
                for u in range(2):
                    if (g, tt // 2) in sorted_x:
                        src = sorted_x[g, tt // 2][:, tt % 2, c, u, :]
                    else:
                        src = words[:, 256 * c + u : 256 * (c + 1) : 2]
                    nc.tensor.transpose(bank[:, 2 * c + u, :], src, ident[:])

        def xcopy(eng, g, tt):
            h = tt // 2
            if (g, h) not in grouped:
                grouped[g, h] = work.tile([P, 2, C, P, 4], BF16, name="xg", tag="xg", align_bytes=256)
            dst = grouped[g, h][:, tt % 2].rearrange("p c r e -> p (c r e)").bitcast(F32).rearrange("p (c r u) -> p c r u", c=C, u=2)
            srcb = banks[g, tt][:].rearrange("p (c u) r -> p c r u", u=2)
            if eng == "v":
                nc.vector.tensor_copy(out=dst, in_=srcb)
            else:
                nc.scalar.copy(out=dst, in_=srcb)

        def xquant(g, h, parts):
            if (g, h) not in xcodes:
                xcodes[g, h] = kept("xc%d%d" % (g, h), [P, 2 * C * P], U32)
                xscale[g, h] = kept("xs%d%d" % (g, h), [P, 2 * C * P], U8)
            w = 2 * C * P // 2
            lo, hi = parts[0] * w, (parts[-1] + 1) * w
            flat = grouped[g, h][:].rearrange("p t c r e -> p (t c r e)")
            nc.vector.quantize_mx(
                out=xcodes[g, h][:, lo:hi].bitcast(FP8X4), scales=xscale[g, h][:, lo:hi], in_=flat[:, 4 * lo : 4 * hi]
            )

        def mm1(g, n, tt):
            bank = acc_pool.tile([P, 512], F32, name="acc", tag="acc")
            banks[g, n, tt] = bank
            for c in range(C):
                lo = ((tt % 2) * C + c) * P
                if n == 0:
                    rhs = bw[:, c, :]
                    rs = wscale[:, C * D + c * K : C * D + (c + 1) * K]
                else:
                    rhs = pw[:, c, 512 * (n - 1) : 512 * n]
                    rs = wscale[:, c * D + 512 * (n - 1) : c * D + 512 * n]
                nc.tensor.matmul_mx(
                    out=bank[:],
                    lhsT=xcodes[g, tt // 2][:, lo : lo + P].bitcast(FP8X4),
                    lhsT_scale=xscale[g, tt // 2][:, lo : lo + P],
                    rhs=rhs.bitcast(FP8X4),
                    rhs_scale=rs,
                    start=(c == 0),
                    stop=(c == C - 1),
                )

        def unit_fused(g, n):
            inter[g, n] = work.tile([P, 512, 4], BF16, name="il", tag="il", align_bytes=256)
            col = (G if n == 0 else 0) + g
            for j in range(4):
                bank = acc_pool.tile([P, 4, P], F32, name="acc", tag="acc")
                for tt in range(4):
                    for c in range(C):
                        lo = ((tt % 2) * C + c) * P
                        if n == 0:
                            rhs = bw[:, c, P * j : P * j + P]
                            off = C * D + c * K + P * j
                        else:
                            rhs = pw[:, c, 512 * (n - 1) + P * j : 512 * (n - 1) + P * j + P]
                            off = c * D + 512 * (n - 1) + P * j
                        nc.tensor.matmul_mx(
                            out=bank[:, tt, :],
                            lhsT=xcodes[g, tt // 2][:, lo : lo + P].bitcast(FP8X4),
                            lhsT_scale=xscale[g, tt // 2][:, lo : lo + P],
                            rhs=rhs.bitcast(FP8X4),
                            rhs_scale=wscale[:, off : off + P],
                            start=(c == 0),
                            stop=(c == C - 1),
                        )
                nc.vector.tensor_tensor(
                    out=inter[g, n][:, P * j : P * j + P, :],
                    in0=bank[:].rearrange("p t n -> p n t"),
                    in1=rt[:, :, col : col + 1].rearrange("p t o -> p o t").to_broadcast([P, P, 4]),
                    op=MULT,
                )

        def evac(eng, g, n, tt):
            if (g, n) not in planes_t:
                planes_t[g, n] = work.tile([P, 4, 512], BF16, name="tb", tag="tb", align_bytes=256)
            dst = planes_t[g, n][:, tt, :]
            col = (G if n == 0 else 0) + g
            fac = rt[:, tt, col : col + 1]
            if eng == "v":
                nc.vector.tensor_scalar(out=dst, in0=banks[g, n, tt][:], scalar1=fac, scalar2=None, op0=MULT)
            else:
                nc.scalar.activation(out=dst, in_=banks[g, n, tt][:], func=COPY, scale=fac)

        def interleave(g, n):
            if (g, n) in FUSED:
                return
            inter[g, n] = work.tile([P, 512, 4], BF16, name="il", tag="il", align_bytes=256)
            nc.vector.tensor_copy(
                out=inter[g, n][:].rearrange("p (c i) t -> p c t i", i=4),
                in_=planes_t[g, n][:].rearrange("p t (c i) -> p c t i", i=4),
            )

        def uquant(g, n):
            ucodes[g, n] = kept("uc%d%d" % (g, n), [P, 512], U32)
            uscale[g, n] = kept("us%d%d" % (g, n), [P, 512], U8)
            nc.vector.quantize_mx(
                out=ucodes[g, n][:].bitcast(FP8X4), scales=uscale[g, n][:], in_=inter[g, n][:].rearrange("p n t -> p (n t)")
            )

        def mm2(m, gs):
            if ("c", m) not in banks:
                banks["c", m] = acc_pool.tile([P, 512], F32, name="acc", tag="acc")
            n = 1 + m // 4
            lo = P * (m % 4)
            for g in gs:
                nc.tensor.matmul_mx(
                    out=banks["c", m][:],
                    lhsT=ucodes[g, n][:, lo : lo + P].bitcast(FP8X4),
                    lhsT_scale=uscale[g, n][:, lo : lo + P],
                    rhs=ucodes[g, 0][:].bitcast(FP8X4),
                    rhs_scale=uscale[g, 0][:],
                    start=(g == 0),
                    stop=(g == G - 1),
                )

        res = {}
        resb = {}
        rgroup = {}

        diff = {}

        def subtract(m):
            diff[m] = work.tile([P, K], F32, name="diff", tag="diff", bufs=4, align_bytes=256)
            nc.vector.scalar_tensor_tensor(
                out=diff[m][:], in0=banks["c", m][:], scalar=1.0 / N, in1=v_sb[:, m, :], op0=MULT, op1=SUB
            )

        def finish(m):
            res[m] = work.tile([P, K], F32, name="res", tag="res", bufs=4, align_bytes=256)
            nc.scalar.activation(out=res[m][:], in_=diff[m][:], func=COPY, scale=rpsi[:, m : m + 1])
            nc.sync.dma_start(out=out[P * m : P * m + P, :], in_=res[m][:])

        def roundr(m):
            resb[m] = work.tile([P, 2, P, 2], BF16, name="resb", tag="resb", bufs=3, align_bytes=256)
            nc.vector.tensor_scalar(
                out=resb[m][:],
                in0=diff[m][:].rearrange("p (k u e) -> p u k e", u=2, e=2),
                scalar1=rpsi[:, m : m + 1],
                scalar2=None,
                op0=MULT,
            )

        def turnr(ms):
            bank = tr_pool.tile([P, len(ms), 2, P], F32, name="trb", tag="trb")
            banks["r", ms[0]] = bank
            for i, m in enumerate(ms):
                words = resb[m][:].rearrange("p u k e -> p (u k e)").bitcast(F32)
                for u in range(2):
                    nc.tensor.transpose(bank[:, i, u, :], words[:, P * u : P * u + P], ident[:])

        def rcopy(ms, eng="s"):
            rgroup[ms[0]] = work.tile([P, len(ms) * P, 4], BF16, name="rg", tag="rg", align_bytes=256)
            dst = (
                rgroup[ms[0]][:].rearrange("p d e -> p (d e)").bitcast(F32)
                .rearrange("p (i d u) -> p i d u", i=len(ms), u=2)
            )
            srcb = banks["r", ms[0]][:].rearrange("p i u d -> p i d u")
            if eng == "v":
                nc.vector.tensor_copy(out=dst, in_=srcb)
            else:
                nc.scalar.copy(out=dst, in_=srcb)

        def rquant(ms):
            cols = slice(P * ms[0], P * ms[-1] + P)
            nc.vector.quantize_mx(
                out=pcodes[:, cols].bitcast(FP8X4), scales=pscale[:, cols], in_=rgroup[ms[0]][:].rearrange("p d e -> p (d e)")
            )

        ow = out_words.rearrange("g p m t -> (g p) (m t)").bitcast(I32)
        os_ = out_scales.rearrange("g q m -> (g q) m").bitcast(I32)

        def store_words(m0, m1):
            nc.sync.dma_start(out=ow[:, P * m0 : P * m1], in_=pcodes[:, P * m0 : P * m1].bitcast(I32))

        def store_scales(m0, m1, engs):
            for q in range(4):
                engs[q].dma_start(
                    out=os_[4 * q : 4 * q + 4, 32 * m0 : 32 * m1],
                    in_=pscale[32 * q : 32 * q + 4, P * m0 : P * m1].bitcast(I32),
                )

        turn(0, 0)
        turn(0, 1)
        turn(0, 2)
        turn(0, 3)
        xcopy("s", 0, 0)
        xcopy("v", 0, 1)
        xquant(0, 0, [0])
        xcopy("s", 0, 2)
        xquant(0, 0, [1])
        xcopy("v", 0, 3)
        mm1(0, 0, 0)
        vt = tr_pool.tile([P, 4, P], BF16, name="trb", tag="trb")
        for tt in range(4):
            nc.tensor.transpose(vt[:, tt, :], vec[:, tt:512:4], ident_bf[:])
        xquant(0, 1, [0])
        nc.vector.tensor_copy(out=rt[:], in_=vt[:, :, 0 : 2 * G])
        xquant(0, 1, [1])
        evac("s", 0, 0, 0)
        for tt in range(1, 4):
            mm1(0, 0, tt)
            evac("s", 0, 0, tt)

        def turn_half(g, h, engs="ss"):
            engs = XC.get((g, h), engs)
            turn(g, 2 * h)
            turn(g, 2 * h + 1)
            xcopy(engs[0], g, 2 * h)
            xcopy(engs[1], g, 2 * h + 1)

        def unit(g, n, tts=range(4)):
            if (g, n) in FUSED:
                unit_fused(g, n)
                return
            for tt in tts:
                mm1(g, n, tt)
                evac("s", g, n, tt)

        sortx("v", 1, 0)
        unit(0, 1)
        interleave(0, 0)
        turn_half(1, 0)
        sortx("v", 1, 1)
        uquant(0, 0)
        unit(0, 2, range(2))
        interleave(0, 1)
        turn_half(1, 1)
        unit(0, 2, range(2, 4))
        xquant(1, 0, [0, 1])
        uquant(0, 1)
        xquant(1, 1, [0, 1])
        sortx("v", 2, 0)
        interleave(0, 2)
        uquant(0, 2)
        for g in range(1, G):
            unit(g, 0)
            if g + 1 < G:
                sortx("v", g + 1, 1)
                turn_half(g + 1, 0)
            interleave(g, 0)
            unit(g, 1)
            uquant(g, 0)
            if g + 1 < G:
                turn_half(g + 1, 1)
                xquant(g + 1, 0, [0, 1])
            interleave(g, 1)
            unit(g, 2)
            if g + 1 < G:
                xquant(g + 1, 1, [0, 1])
            uquant(g, 1)
            if g + 2 < G:
                sortx("v", g + 2, 0)
            interleave(g, 2)
            if g == 2:
                psi_t = tr_pool.tile([P, P], BF16, name="trb", tag="trb")
                nc.tensor.transpose(psi_t[:], psi_sb[:], ident_bf[:])
                nc.vector.reciprocal(out=rpsi[:], in_=psi_t[:, 0:MT])
            uquant(g, 2)

        for m in range(3):
            mm2(m, range(G - 1))
        for m in range(3):
            mm2(m, [G - 1])
            subtract(m)
            finish(m)
        mm2(3, range(G))
        roundr(0)
        roundr(1)
        subtract(3)
        finish(3)
        mm2(4, range(G))
        turnr([0, 1])
        roundr(2)
        rcopy([0, 1])
        subtract(4)
        roundr(3)
        finish(4)
        mm2(5, range(G))
        rquant([0, 1])
        store_words(0, 2)
        turnr([2, 3])
        rcopy([2, 3])
        roundr(4)
        subtract(5)
        finish(5)
        roundr(5)
        rquant([2, 3])
        store_words(2, 4)
        store_scales(0, 4, [nc.sync] * 4)
        mm2(6, range(G))
        turnr([4, 5])
        rcopy([4, 5])
        subtract(6)
        roundr(6)
        finish(6)
        mm2(7, range(G))
        turnr([6])
        rcopy([6])
        subtract(7)
        finish(7)
        rquant([4, 5])
        store_words(4, 6)
        roundr(7)
        rquant([6])
        turnr([7])
        rcopy([7])
        rquant([7])
        store_words(6, 8)
        store_scales(4, 8, [nc.sync, nc.scalar, nc.sync, nc.scalar])
